import numpy as np
import ml_dtypes


def mxq(x, axis, fmt="e4m3"):
    dtype, down = {"e4m3": (ml_dtypes.float8_e4m3fn, 7), "e5m2": (ml_dtypes.float8_e5m2, 14)}[fmt]
    v = np.moveaxis(np.asarray(x, np.float32).astype(ml_dtypes.bfloat16).astype(np.float64), axis, -1)
    blocks = v.reshape(v.shape[:-1] + (-1, 32))
    amax = np.abs(blocks).max(-1, keepdims=True)
    byte = np.maximum(np.where(amax > 0, np.frexp(amax)[1] - 1 + 127, 0) - down, 1)
    scale = np.exp2(byte - 127.0)
    codes = (blocks / scale).astype(np.float32).astype(dtype).astype(np.float64)
    return np.moveaxis((codes * scale).reshape(v.shape), -1, axis)


WIDE = False


def mx_kscale(k):
    if not WIDE:
        return np.ones(k)
    levels = np.array([10, -10, 5, -5, 0])
    if k % 512:
        return np.exp2(np.random.permutation(np.resize(levels, k // 32))).repeat(32)
    a = np.empty((k // 512, 16))
    for p in range(k // 512):
        a[p, :8] = np.random.permutation(np.resize(levels, 8))
        for g in range(8):
            far = levels[np.abs(levels - a[p, g]) >= 10]
            a[p, g + 8] = far[np.random.randint(len(far))]
    return np.exp2(a.ravel()).repeat(32)


def f64(x):
    return np.asarray(x).astype(np.float64)


def striped8(idx):
    return np.asarray(idx).reshape(8, -1, 16).transpose(0, 2, 1).reshape(128, -1).astype(np.uint16)


def unstriped8(offs):
    return offs.reshape(8, 16, -1).transpose(0, 2, 1).reshape(8, -1).astype(np.int64)


def pick8(x, idx, run):
    r = np.arange(len(x))
    return x[r[:, None], idx[r % (8 * run) // run]]


E2M1 = np.array([0.0, 0.5, 1.0, 1.5, 2.0, 3.0, 4.0, 6.0, -0.0, -0.5, -1.0, -1.5, -2.0, -3.0, -4.0, -6.0])


def pack_weight(w, fmt):
    k, n = w.shape
    w = f64(np.asarray(w, np.float32).astype(ml_dtypes.bfloat16)).reshape(k // 32, 32, n)
    amax = np.abs(w).max(1)
    if fmt == "e4m3":
        byte = np.frexp(amax)[1] - 1 + 127 - 7
    else:
        mant, ex = np.frexp(amax / 6.0)
        byte = np.where(mant > 0.5, ex, ex - 1) + 127
    byte = np.clip(np.where(amax > 0, byte, 1), 1, 254)
    scaled = (w * np.exp2(127.0 - byte)[:, None, :]).reshape(k, n).astype(np.float32)
    by_word = np.ascontiguousarray(scaled.reshape(k // 512, 128, 4, n).transpose(0, 1, 3, 2))
    if fmt == "e4m3":
        words = by_word.astype(ml_dtypes.float8_e4m3fn).view(np.uint8)
    else:
        c = by_word.astype(ml_dtypes.float4_e2m1fn).view(np.uint8) & 0xF
        words = (c[..., 0::2] | (c[..., 1::2] << 4)).reshape(k // 512, 128, 2 * n)
    return np.ascontiguousarray(words), np.ascontiguousarray(byte.astype(np.uint8).reshape(k // 512, 16, n))


def unpack_weight(words, scales, fmt):
    g, _, n = scales.shape
    words = np.ascontiguousarray(words).reshape(g, 128, n, -1)
    if fmt == "e4m3":
        vals = words.view(ml_dtypes.float8_e4m3fn).astype(np.float64)
    else:
        nib = np.empty((g, 128, n, 4), np.uint8)
        nib[..., 0::2] = words & 0xF
        nib[..., 1::2] = words >> 4
        vals = E2M1[nib]
    vals = vals * np.repeat(np.exp2(scales.astype(np.float64) - 127.0), 8, axis=1)[..., None]
    return vals.transpose(0, 1, 3, 2).reshape(g * 512, n)


D, T, I, Q = 512, 1024, 512, 128


def setup_inputs():
    n = np.random.standard_normal
    idx = np.stack([np.random.permutation(T)[:I] for _ in range(8)])
    idx2 = np.stack([np.random.permutation(T)[:I] for _ in range(8)])
    idx3 = np.stack([np.random.permutation(T)[:I] for _ in range(8)])
    fd = mx_kscale(D)
    keysp = pack_weight(n((D, T)) / fd[:, None], "e2m1")
    return {
        "query": (n((D, Q)) * 1.0 / np.sqrt(D) * fd[:, None]).astype(np.float32),
        "keys_words": keysp[0],
        "keys_scales": keysp[1],
        "offs": striped8(idx),
        "offs2": striped8(idx2),
        "offs3": striped8(idx3),
    }


def reference(query, keys_words, keys_scales, offs, offs2, offs3):
    idx = unstriped8(offs)
    idx2 = unstriped8(offs2)
    idx3 = unstriped8(offs3)
    keysu = unpack_weight(keys_words, keys_scales, "e2m1")
    queryq = mxq(f64(query), 0, "e4m3")
    a = queryq.T @ keysu
    r = pick8(a, idx2, 16) - pick8(a, idx, 16)
    f1 = np.zeros((Q, T))
    f1[np.arange(Q)[:, None], idx[np.arange(Q) % 128 // 16]] = r
    f2 = np.zeros((Q, T))
    f2[np.arange(Q)[:, None], idx2[np.arange(Q) % 128 // 16]] = r
    c1 = a + f1
    c2 = c1 - f2
    y = pick8(c2, idx3, 16)
    return y

@@ -1,0 +1,135 @@
+from contextlib import ExitStack
+
+import concourse.mybir as mybir
+from concourse.masks import make_identity
+
+D, T, I, Q = 512, 1024, 512, 128
+FLOPS = 2 * D * T * Q
+
+F32 = mybir.dt.float32
+BF16 = mybir.dt.bfloat16
+I32 = mybir.dt.int32
+U32 = mybir.dt.uint32
+U16 = mybir.dt.uint16
+U8 = mybir.dt.uint8
+FP8X4 = mybir.dt.float8_e4m3fn_x4
+FP4X4 = mybir.dt.float4_e2m1fn_x4
+ADD = mybir.AluOpType.add
+SUB = mybir.AluOpType.subtract
+COPY = mybir.ActivationFunctionType.Copy
+
+P = 128
+PACK = 4
+N_MM = 256
+BANK = 512
+HALF = I // 2
+LIST_COLS = I // 16
+
+
+def tile_attend_swapped_one_kernel(tc, query, keys_words, keys_scales, offs, offs2, offs3, out):
+    nc = tc.nc
+    with ExitStack() as ctx:
+        lists = ctx.enter_context(tc.tile_pool(name="lists", bufs=1))
+        sb = ctx.enter_context(tc.tile_pool(name="sb", bufs=1))
+        ps = ctx.enter_context(tc.psum_pool(name="ps", bufs=1))
+
+        idx1 = lists.tile([P, LIST_COLS], U16, name="idx1")
+        idx2 = lists.tile([P, LIST_COLS], U16, name="idx2")
+        idx3 = lists.tile([P, LIST_COLS], U16, name="idx3")
+
+        q_raw = sb.tile([P, PACK, Q], F32, name="q_raw")
+        k_words = sb.tile([P, 2 * T], U8, name="k_words", align_bytes=64)
+        k_scales = sb.tile([P, T], U8, name="k_scales", align_bytes=64)
+
+        nc.sync.dma_start(out=q_raw[:], in_=query.rearrange("(p j) q -> p j q", j=PACK))
+        nc.sync.dma_start(out=k_words[:], in_=keys_words[0])
+        nc.vector.memset(k_scales[:].bitcast(I32), 0)
+        for quad in range(4):
+            nc.scalar.dma_start(
+                out=k_scales[32 * quad : 32 * quad + 4, :].bitcast(I32),
+                in_=keys_scales[0, 4 * quad : 4 * quad + 4, :].bitcast(I32),
+            )
+        nc.sync.dma_start(idx1[:], offs)
+        nc.sync.dma_start(idx2[:], offs2)
+        nc.sync.dma_start(idx3[:], offs3)
+
+        f1 = sb.tile([P, T], F32, name="f1")
+        f2 = sb.tile([P, T], F32, name="f2")
+        nc.vector.memset(f1[:], 0.0)
+        nc.vector.memset(f2[:], 0.0)
+        ident = sb.tile([P, P], F32, name="ident")
+        make_identity(nc, ident[:])
+
+        q_bf = sb.tile([P, Q, PACK], BF16, name="q_bf", align_bytes=64)
+        nc.vector.tensor_copy(out=q_bf[:], in_=q_raw[:].rearrange("p j q -> p q j"))
+        q_codes = sb.tile([P, Q], U32, name="q_codes", align_bytes=64)
+        q_scales = sb.tile([P, Q], U8, name="q_scales", align_bytes=64)
+        nc.vector.quantize_mx(
+            out=q_codes[:].bitcast(FP8X4),
+            scales=q_scales[:],
+            in_=q_bf[:].rearrange("p q j -> p (q j)"),
+        )
+
+        a = sb.tile([P, T], F32, name="a")
+        for c in range(T // N_MM):
+            cols = slice(c * N_MM, (c + 1) * N_MM)
+            acc = ps.tile([P, N_MM], F32, name="acc%d" % c)
+            nc.tensor.matmul_mx(
+                out=acc[:],
+                lhsT=q_codes[:].bitcast(FP8X4),
+                lhsT_scale=q_scales[:],
+                rhs=k_words[:, 2 * cols.start : 2 * cols.stop].bitcast(FP4X4),
+                rhs_scale=k_scales[:, cols],
+                start=True,
+                stop=True,
+            )
+            if c % 2 == 0:
+                nc.scalar.copy(out=a[:, cols], in_=acc[:])
+            else:
+                nc.vector.tensor_copy(out=a[:, cols], in_=acc[:])
+
+        first, second = slice(0, HALF), slice(HALF, I)
+        first_l, second_l = slice(0, LIST_COLS // 2), slice(LIST_COLS // 2, LIST_COLS)
+        at2 = sb.tile([P, I], F32, name="at2")
+        neg_at1 = sb.tile([P, I], F32, name="neg_at1")
+        nc.vector.tensor_copy(out=at2[:, first], in_=a[:].indirect(idx2[:, first_l]))
+        nc.scalar.activation(neg_at1[:, first], a[:].indirect(idx1[:, first_l]), COPY, scale=-1.0)
+        nc.scalar.activation(at2[:, second], a[:].indirect(idx2[:, second_l]), COPY)
+        nc.scalar.activation(neg_at1[:, second], a[:].indirect(idx1[:, second_l]), COPY, scale=-1.0)
+
+        nc.vector.tensor_tensor(f1[:].indirect(idx1[:, first_l]), at2[:, first], neg_at1[:, first], ADD)
+        nc.vector.tensor_tensor(f1[:].indirect(idx1[:, second_l]), at2[:, second], neg_at1[:, second], ADD)
+        nc.vector.tensor_tensor(f2[:].indirect(idx2[:]), at2[:], neg_at1[:], ADD)
+
+        blocks = BANK // P
+        c1_t = sb.tile([P, T], F32, name="c1_t")
+        c2 = sb.tile([P, T], F32, name="c2")
+        sums = [ps.tile([P, BANK], F32, name="sum%d" % b) for b in range(T // BANK)]
+        c1 = [ps.tile([P, BANK], F32, name="c1_%d" % b) for b in range(T // BANK)]
+        for term, source in enumerate((a, f1)):
+            for b in range(T // BANK):
+                for j in range(blocks):
+                    col = b * BANK + j * P
+                    nc.tensor.matmul(
+                        sums[b][:, j * P : (j + 1) * P],
+                        source[:, col : col + P],
+                        ident[:],
+                        start=(term == 0 and j == 0),
+                        stop=(term == 1 and j == blocks - 1),
+                        is_transpose=True,
+                    )
+        for b in range(T // BANK):
+            nc.scalar.copy(out=c1_t[:, b * BANK : (b + 1) * BANK], in_=sums[b][:])
+            for j in range(blocks):
+                col = b * BANK + j * P
+                nc.tensor.transpose(c1[b][:, j * P : (j + 1) * P], c1_t[:, col : col + P], ident[:])
+        for b in range(T // BANK):
+            cols = slice(b * BANK, (b + 1) * BANK)
+            nc.vector.tensor_tensor(c2[:, cols], c1[b][:], f2[:, cols], SUB)
+
+        y0 = sb.tile([P, HALF], F32, name="y0")
+        y1 = sb.tile([P, HALF], F32, name="y1")
+        nc.vector.tensor_copy(out=y0[:], in_=c2[:].indirect(idx3[:, first_l]))
+        nc.scalar.activation(y1[:], c2[:].indirect(idx3[:, second_l]), COPY)
+        nc.sync.dma_start(out=out[:, first], in_=y0[:])
+        nc.scalar.dma_start(out=out[:, second], in_=y1[:])

@@ -20,10 +20,12 @@ COPY = mybir.ActivationFunctionType.Copy
 
 P = 128
 PACK = 4
-N_MM = 256
+WIDTHS = (256, 256, 256, 128, 128)
 BANK = 512
+GROUP = 256
 HALF = I // 2
 LIST_COLS = I // 16
+Q_VECTOR = 56
 
 
 def tile_attend_swapped_one_kernel(tc, query, keys_words, keys_scales, offs, offs2, offs3, out):
@@ -38,14 +40,14 @@ def tile_attend_swapped_one_kernel(tc, query, keys_words, keys_scales, offs, off
         idx3 = lists.tile([P, LIST_COLS], U16, name="idx3")
 
         q_raw = sb.tile([P, PACK, Q], F32, name="q_raw")
-        k_words = sb.tile([P, 2 * T], U8, name="k_words", align_bytes=64)
+        k_words = sb.tile([P, 2 * T], U8, name="k_words", tag="k_words", align_bytes=64)
         k_scales = sb.tile([P, T], U8, name="k_scales", align_bytes=64)
 
         nc.sync.dma_start(out=q_raw[:], in_=query.rearrange("(p j) q -> p j q", j=PACK))
         nc.sync.dma_start(out=k_words[:], in_=keys_words[0])
         nc.vector.memset(k_scales[:].bitcast(I32), 0)
         for quad in range(4):
-            nc.scalar.dma_start(
+            nc.sync.dma_start(
                 out=k_scales[32 * quad : 32 * quad + 4, :].bitcast(I32),
                 in_=keys_scales[0, 4 * quad : 4 * quad + 4, :].bitcast(I32),
             )
@@ -53,15 +55,15 @@ def tile_attend_swapped_one_kernel(tc, query, keys_words, keys_scales, offs, off
         nc.sync.dma_start(idx2[:], offs2)
         nc.sync.dma_start(idx3[:], offs3)
 
-        f1 = sb.tile([P, T], F32, name="f1")
-        f2 = sb.tile([P, T], F32, name="f2")
-        nc.vector.memset(f1[:], 0.0)
-        nc.vector.memset(f2[:], 0.0)
+        f1_first = sb.tile([P, T], F32, name="f1_first")
+        nc.vector.memset(f1_first[:], 0.0)
         ident = sb.tile([P, P], F32, name="ident")
         make_identity(nc, ident[:])
 
-        q_bf = sb.tile([P, Q, PACK], BF16, name="q_bf", align_bytes=64)
-        nc.vector.tensor_copy(out=q_bf[:], in_=q_raw[:].rearrange("p j q -> p q j"))
+        q_bf = sb.tile([P, Q, PACK], BF16, name="q_bf", tag="q_bf", align_bytes=64)
+        q_turned = q_raw[:].rearrange("p j q -> p q j")
+        nc.vector.tensor_copy(out=q_bf[:, :Q_VECTOR, :], in_=q_turned[:, :Q_VECTOR, :])
+        nc.scalar.copy(out=q_bf[:, Q_VECTOR:, :], in_=q_turned[:, Q_VECTOR:, :])
         q_codes = sb.tile([P, Q], U32, name="q_codes", align_bytes=64)
         q_scales = sb.tile([P, Q], U8, name="q_scales", align_bytes=64)
         nc.vector.quantize_mx(
@@ -70,10 +72,15 @@ def tile_attend_swapped_one_kernel(tc, query, keys_words, keys_scales, offs, off
             in_=q_bf[:].rearrange("p q j -> p (q j)"),
         )
 
+        f2 = sb.tile([P, T], F32, name="f2", tag="q_bf", align_bytes=64)
+        nc.gpsimd.memset(f2[:], 0.0)
+
         a = sb.tile([P, T], F32, name="a")
-        for c in range(T // N_MM):
-            cols = slice(c * N_MM, (c + 1) * N_MM)
-            acc = ps.tile([P, N_MM], F32, name="acc%d" % c)
+        start = 0
+        for c, width in enumerate(WIDTHS):
+            cols = slice(start, start + width)
+            start = cols.stop
+            acc = ps.tile([P, width], F32, name="acc%d" % c, tag="bank%d" % c)
             nc.tensor.matmul_mx(
                 out=acc[:],
                 lhsT=q_codes[:].bitcast(FP8X4),
@@ -88,6 +95,10 @@ def tile_attend_swapped_one_kernel(tc, query, keys_words, keys_scales, offs, off
             else:
                 nc.vector.tensor_copy(out=a[:, cols], in_=acc[:])
 
+        f1_second = sb.tile([P, T], F32, name="f1_second", tag="k_words", align_bytes=64)
+        nc.gpsimd.memset(f1_second[:], 0.0)
+        f1 = (f1_first, f1_second)
+
         first, second = slice(0, HALF), slice(HALF, I)
         first_l, second_l = slice(0, LIST_COLS // 2), slice(LIST_COLS // 2, LIST_COLS)
         at2 = sb.tile([P, I], F32, name="at2")
@@ -97,35 +108,36 @@ def tile_attend_swapped_one_kernel(tc, query, keys_words, keys_scales, offs, off
         nc.scalar.activation(at2[:, second], a[:].indirect(idx2[:, second_l]), COPY)
         nc.scalar.activation(neg_at1[:, second], a[:].indirect(idx1[:, second_l]), COPY, scale=-1.0)
 
-        nc.vector.tensor_tensor(f1[:].indirect(idx1[:, first_l]), at2[:, first], neg_at1[:, first], ADD)
-        nc.vector.tensor_tensor(f1[:].indirect(idx1[:, second_l]), at2[:, second], neg_at1[:, second], ADD)
+        nc.vector.tensor_tensor(f1[0][:].indirect(idx1[:, first_l]), at2[:, first], neg_at1[:, first], ADD)
+        nc.vector.tensor_tensor(f1[1][:].indirect(idx1[:, second_l]), at2[:, second], neg_at1[:, second], ADD)
         nc.vector.tensor_tensor(f2[:].indirect(idx2[:]), at2[:], neg_at1[:], ADD)
 
-        blocks = BANK // P
+        groups, blocks = T // GROUP, GROUP // P
         c1_t = sb.tile([P, T], F32, name="c1_t")
         c2 = sb.tile([P, T], F32, name="c2")
-        sums = [ps.tile([P, BANK], F32, name="sum%d" % b) for b in range(T // BANK)]
-        c1 = [ps.tile([P, BANK], F32, name="c1_%d" % b) for b in range(T // BANK)]
-        for term, source in enumerate((a, f1)):
-            for b in range(T // BANK):
+        sums = [ps.tile([P, GROUP], F32, name="sum%d" % g, tag="bank%d" % g) for g in range(groups)]
+        terms = (a, f1[0], f1[1])
+        for term, source in enumerate(terms):
+            for g in range(groups):
                 for j in range(blocks):
-                    col = b * BANK + j * P
+                    col = g * GROUP + j * P
                     nc.tensor.matmul(
-                        sums[b][:, j * P : (j + 1) * P],
+                        sums[g][:, j * P : (j + 1) * P],
                         source[:, col : col + P],
                         ident[:],
                         start=(term == 0 and j == 0),
-                        stop=(term == 1 and j == blocks - 1),
+                        stop=(term == len(terms) - 1 and j == blocks - 1),
                         is_transpose=True,
                     )
-        for b in range(T // BANK):
-            nc.scalar.copy(out=c1_t[:, b * BANK : (b + 1) * BANK], in_=sums[b][:])
-            for j in range(blocks):
-                col = b * BANK + j * P
-                nc.tensor.transpose(c1[b][:, j * P : (j + 1) * P], c1_t[:, col : col + P], ident[:])
-        for b in range(T // BANK):
-            cols = slice(b * BANK, (b + 1) * BANK)
-            nc.vector.tensor_tensor(c2[:, cols], c1[b][:], f2[:, cols], SUB)
+        spans = (slice(0, BANK), slice(BANK, T))
+        c1 = [ps.tile([P, s.stop - s.start], F32, name="c1_%d" % s.start) for s in spans]
+        for g in range(groups):
+            nc.scalar.copy(out=c1_t[:, g * GROUP : (g + 1) * GROUP], in_=sums[g][:])
+        for span, bank in zip(spans, c1):
+            for col in range(span.start, span.stop, P):
+                nc.tensor.transpose(bank[:, col - span.start : col - span.start + P], c1_t[:, col : col + P], ident[:])
+        for span, bank in zip(spans, c1):
+            nc.vector.tensor_tensor(c2[:, span], bank[:], f2[:, span], SUB)
 
         y0 = sb.tile([P, HALF], F32, name="y0")
         y1 = sb.tile([P, HALF], F32, name="y1")

@@ -72,8 +72,8 @@ def tile_attend_swapped_one_kernel(tc, query, keys_words, keys_scales, offs, off
             in_=q_bf[:].rearrange("p q j -> p (q j)"),
         )
 
-        f2 = sb.tile([P, T], F32, name="f2", tag="q_bf", align_bytes=64)
-        nc.gpsimd.memset(f2[:], 0.0)
+        f1_second = sb.tile([P, T], F32, name="f1_second", tag="q_bf", align_bytes=64)
+        nc.gpsimd.memset(f1_second[:], 0.0)
 
         a = sb.tile([P, T], F32, name="a")
         start = 0
@@ -95,8 +95,8 @@ def tile_attend_swapped_one_kernel(tc, query, keys_words, keys_scales, offs, off
             else:
                 nc.vector.tensor_copy(out=a[:, cols], in_=acc[:])
 
-        f1_second = sb.tile([P, T], F32, name="f1_second", tag="k_words", align_bytes=64)
-        nc.gpsimd.memset(f1_second[:], 0.0)
+        f2 = sb.tile([P, T], F32, name="f2", tag="k_words", align_bytes=64)
+        nc.gpsimd.memset(f2[:], 0.0)
         f1 = (f1_first, f1_second)
 
         first, second = slice(0, HALF), slice(HALF, I)
@@ -129,14 +129,17 @@ def tile_attend_swapped_one_kernel(tc, query, keys_words, keys_scales, offs, off
                         stop=(term == len(terms) - 1 and j == blocks - 1),
                         is_transpose=True,
                     )
-        spans = (slice(0, BANK), slice(BANK, T))
+        spans = (slice(0, GROUP), slice(GROUP, BANK), slice(BANK, T))
         c1 = [ps.tile([P, s.stop - s.start], F32, name="c1_%d" % s.start) for s in spans]
         for g in range(groups):
             nc.scalar.copy(out=c1_t[:, g * GROUP : (g + 1) * GROUP], in_=sums[g][:])
         for span, bank in zip(spans, c1):
             for col in range(span.start, span.stop, P):
                 nc.tensor.transpose(bank[:, col - span.start : col - span.start + P], c1_t[:, col : col + P], ident[:])
-        for span, bank in zip(spans, c1):
+        c1_head = sb.tile([P, GROUP], F32, name="c1_head")
+        nc.scalar.copy(out=c1_head[:], in_=c1[0][:])
+        nc.gpsimd.tensor_tensor(c2[:, spans[0]], c1_head[:], f2[:, spans[0]], SUB)
+        for span, bank in zip(spans[1:], c1[1:]):
             nc.vector.tensor_tensor(c2[:, span], bank[:], f2[:, span], SUB)
 
         y0 = sb.tile([P, HALF], F32, name="y0")

@@ -40,7 +40,7 @@ def tile_attend_swapped_one_kernel(tc, query, keys_words, keys_scales, offs, off
         idx3 = lists.tile([P, LIST_COLS], U16, name="idx3")
 
         q_raw = sb.tile([P, PACK, Q], F32, name="q_raw")
-        k_words = sb.tile([P, 2 * T], U8, name="k_words", tag="k_words", align_bytes=64)
+        k_words = sb.tile([P, 2 * T], U8, name="k_words", align_bytes=64)
         k_scales = sb.tile([P, T], U8, name="k_scales", align_bytes=64)
 
         nc.sync.dma_start(out=q_raw[:], in_=query.rearrange("(p j) q -> p j q", j=PACK))
@@ -55,8 +55,9 @@ def tile_attend_swapped_one_kernel(tc, query, keys_words, keys_scales, offs, off
         nc.sync.dma_start(idx2[:], offs2)
         nc.sync.dma_start(idx3[:], offs3)
 
-        f1_first = sb.tile([P, T], F32, name="f1_first")
-        nc.vector.memset(f1_first[:], 0.0)
+        f1 = [sb.tile([P, T], F32, name="f1_%d" % h) for h in range(2)]
+        for window in f1:
+            nc.vector.memset(window[:], 0.0)
         ident = sb.tile([P, P], F32, name="ident")
         make_identity(nc, ident[:])
 
@@ -72,8 +73,8 @@ def tile_attend_swapped_one_kernel(tc, query, keys_words, keys_scales, offs, off
             in_=q_bf[:].rearrange("p q j -> p (q j)"),
         )
 
-        f1_second = sb.tile([P, T], F32, name="f1_second", tag="q_bf", align_bytes=64)
-        nc.gpsimd.memset(f1_second[:], 0.0)
+        f2 = sb.tile([P, T], F32, name="f2", tag="q_bf", align_bytes=64)
+        nc.gpsimd.memset(f2[:], 0.0)
 
         a = sb.tile([P, T], F32, name="a")
         start = 0
@@ -94,10 +95,6 @@ def tile_attend_swapped_one_kernel(tc, query, keys_words, keys_scales, offs, off
                 nc.scalar.copy(out=a[:, cols], in_=acc[:])
             else:
                 nc.vector.tensor_copy(out=a[:, cols], in_=acc[:])
-
-        f2 = sb.tile([P, T], F32, name="f2", tag="k_words", align_bytes=64)
-        nc.gpsimd.memset(f2[:], 0.0)
-        f1 = (f1_first, f1_second)
 
         first, second = slice(0, HALF), slice(HALF, I)
         first_l, second_l = slice(0, LIST_COLS // 2), slice(LIST_COLS // 2, LIST_COLS)
@@ -129,14 +126,14 @@ def tile_attend_swapped_one_kernel(tc, query, keys_words, keys_scales, offs, off
                         stop=(term == len(terms) - 1 and j == blocks - 1),
                         is_transpose=True,
                     )
-        spans = (slice(0, GROUP), slice(GROUP, BANK), slice(BANK, T))
+        spans = (slice(0, 384), slice(384, BANK), slice(BANK, T))
         c1 = [ps.tile([P, s.stop - s.start], F32, name="c1_%d" % s.start) for s in spans]
         for g in range(groups):
             nc.scalar.copy(out=c1_t[:, g * GROUP : (g + 1) * GROUP], in_=sums[g][:])
         for span, bank in zip(spans, c1):
             for col in range(span.start, span.stop, P):
                 nc.tensor.transpose(bank[:, col - span.start : col - span.start + P], c1_t[:, col : col + P], ident[:])
-        c1_head = sb.tile([P, GROUP], F32, name="c1_head")
+        c1_head = sb.tile([P, 384], F32, name="c1_head")
         nc.scalar.copy(out=c1_head[:], in_=c1[0][:])
         nc.gpsimd.tensor_tensor(c2[:, spans[0]], c1_head[:], f2[:, spans[0]], SUB)
         for span, bank in zip(spans[1:], c1[1:]):

from contextlib import ExitStack

import concourse.mybir as mybir
from concourse.masks import make_identity

D, T, I, Q = 512, 1024, 512, 128
FLOPS = 2 * D * T * Q

F32 = mybir.dt.float32
BF16 = mybir.dt.bfloat16
I32 = mybir.dt.int32
U32 = mybir.dt.uint32
U16 = mybir.dt.uint16
U8 = mybir.dt.uint8
FP8X4 = mybir.dt.float8_e4m3fn_x4
FP4X4 = mybir.dt.float4_e2m1fn_x4
ADD = mybir.AluOpType.add
SUB = mybir.AluOpType.subtract
COPY = mybir.ActivationFunctionType.Copy

P = 128
PACK = 4
WIDTHS = (256, 256, 256, 128, 128)
BANK = 512
GROUP = 256
HALF = I // 2
LIST_COLS = I // 16
Q_VECTOR = 56


def tile_attend_swapped_one_kernel(tc, query, keys_words, keys_scales, offs, offs2, offs3, out):
    nc = tc.nc
    with ExitStack() as ctx:
        lists = ctx.enter_context(tc.tile_pool(name="lists", bufs=1))
        sb = ctx.enter_context(tc.tile_pool(name="sb", bufs=1))
        ps = ctx.enter_context(tc.psum_pool(name="ps", bufs=1))

        idx1 = lists.tile([P, LIST_COLS], U16, name="idx1")
        idx2 = lists.tile([P, LIST_COLS], U16, name="idx2")
        idx3 = lists.tile([P, LIST_COLS], U16, name="idx3")

        q_raw = sb.tile([P, PACK, Q], F32, name="q_raw")
        k_words = sb.tile([P, 2 * T], U8, name="k_words", align_bytes=64)
        k_scales = sb.tile([P, T], U8, name="k_scales", align_bytes=64)

        nc.sync.dma_start(out=q_raw[:], in_=query.rearrange("(p j) q -> p j q", j=PACK))
        nc.sync.dma_start(out=k_words[:], in_=keys_words[0])
        nc.vector.memset(k_scales[:].bitcast(I32), 0)
        for quad in range(4):
            nc.sync.dma_start(
                out=k_scales[32 * quad : 32 * quad + 4, :].bitcast(I32),
                in_=keys_scales[0, 4 * quad : 4 * quad + 4, :].bitcast(I32),
            )
        nc.sync.dma_start(idx1[:], offs)
        nc.sync.dma_start(idx2[:], offs2)
        nc.sync.dma_start(idx3[:], offs3)

        f1 = [sb.tile([P, T], F32, name="f1_%d" % h) for h in range(2)]
        for window in f1:
            nc.vector.memset(window[:], 0.0)
        ident = sb.tile([P, P], F32, name="ident")
        make_identity(nc, ident[:])

        q_bf = sb.tile([P, Q, PACK], BF16, name="q_bf", tag="q_bf", align_bytes=64)
        q_turned = q_raw[:].rearrange("p j q -> p q j")
        nc.vector.tensor_copy(out=q_bf[:, :Q_VECTOR, :], in_=q_turned[:, :Q_VECTOR, :])
        nc.scalar.copy(out=q_bf[:, Q_VECTOR:, :], in_=q_turned[:, Q_VECTOR:, :])
        q_codes = sb.tile([P, Q], U32, name="q_codes", align_bytes=64)
        q_scales = sb.tile([P, Q], U8, name="q_scales", align_bytes=64)
        nc.vector.quantize_mx(
            out=q_codes[:].bitcast(FP8X4),
            scales=q_scales[:],
            in_=q_bf[:].rearrange("p q j -> p (q j)"),
        )

        f2 = sb.tile([P, T], F32, name="f2", tag="q_bf", align_bytes=64)
        nc.gpsimd.memset(f2[:], 0.0)

        a = sb.tile([P, T], F32, name="a")
        start = 0
        for c, width in enumerate(WIDTHS):
            cols = slice(start, start + width)
            start = cols.stop
            acc = ps.tile([P, width], F32, name="acc%d" % c, tag="bank%d" % c)
            nc.tensor.matmul_mx(
                out=acc[:],
                lhsT=q_codes[:].bitcast(FP8X4),
                lhsT_scale=q_scales[:],
                rhs=k_words[:, 2 * cols.start : 2 * cols.stop].bitcast(FP4X4),
                rhs_scale=k_scales[:, cols],
                start=True,
                stop=True,
            )
            if c % 2 == 0:
                nc.scalar.copy(out=a[:, cols], in_=acc[:])
            else:
                nc.vector.tensor_copy(out=a[:, cols], in_=acc[:])

        first, second = slice(0, HALF), slice(HALF, I)
        first_l, second_l = slice(0, LIST_COLS // 2), slice(LIST_COLS // 2, LIST_COLS)
        at2 = sb.tile([P, I], F32, name="at2")
        neg_at1 = sb.tile([P, I], F32, name="neg_at1")
        nc.vector.tensor_copy(out=at2[:, first], in_=a[:].indirect(idx2[:, first_l]))
        nc.scalar.activation(neg_at1[:, first], a[:].indirect(idx1[:, first_l]), COPY, scale=-1.0)
        nc.scalar.activation(at2[:, second], a[:].indirect(idx2[:, second_l]), COPY)
        nc.scalar.activation(neg_at1[:, second], a[:].indirect(idx1[:, second_l]), COPY, scale=-1.0)

        nc.vector.tensor_tensor(f1[0][:].indirect(idx1[:, first_l]), at2[:, first], neg_at1[:, first], ADD)
        nc.vector.tensor_tensor(f1[1][:].indirect(idx1[:, second_l]), at2[:, second], neg_at1[:, second], ADD)
        nc.vector.tensor_tensor(f2[:].indirect(idx2[:]), at2[:], neg_at1[:], ADD)

        groups, blocks = T // GROUP, GROUP // P
        c1_t = sb.tile([P, T], F32, name="c1_t")
        c2 = sb.tile([P, T], F32, name="c2")
        sums = [ps.tile([P, GROUP], F32, name="sum%d" % g, tag="bank%d" % g) for g in range(groups)]
        terms = (a, f1[0], f1[1])
        for term, source in enumerate(terms):
            for g in range(groups):
                for j in range(blocks):
                    col = g * GROUP + j * P
                    nc.tensor.matmul(
                        sums[g][:, j * P : (j + 1) * P],
                        source[:, col : col + P],
                        ident[:],
                        start=(term == 0 and j == 0),
                        stop=(term == len(terms) - 1 and j == blocks - 1),
                        is_transpose=True,
                    )
        spans = (slice(0, 384), slice(384, BANK), slice(BANK, T))
        c1 = [ps.tile([P, s.stop - s.start], F32, name="c1_%d" % s.start) for s in spans]
        for g in range(groups):
            nc.scalar.copy(out=c1_t[:, g * GROUP : (g + 1) * GROUP], in_=sums[g][:])
        for span, bank in zip(spans, c1):
            for col in range(span.start, span.stop, P):
                nc.tensor.transpose(bank[:, col - span.start : col - span.start + P], c1_t[:, col : col + P], ident[:])
        c1_head = sb.tile([P, 384], F32, name="c1_head")
        nc.scalar.copy(out=c1_head[:], in_=c1[0][:])
        nc.gpsimd.tensor_tensor(c2[:, spans[0]], c1_head[:], f2[:, spans[0]], SUB)
        for span, bank in zip(spans[1:], c1[1:]):
            nc.vector.tensor_tensor(c2[:, span], bank[:], f2[:, span], SUB)

        y0 = sb.tile([P, HALF], F32, name="y0")
        y1 = sb.tile([P, HALF], F32, name="y1")
        nc.vector.tensor_copy(out=y0[:], in_=c2[:].indirect(idx3[:, first_l]))
        nc.scalar.activation(y1[:], c2[:].indirect(idx3[:, second_l]), COPY)
        nc.sync.dma_start(out=out[:, first], in_=y0[:])
        nc.scalar.dma_start(out=out[:, second], in_=y1[:])
